import numpy as np
CORES = [30,54,78,102,158,182,206,230,286,310,334,358,414,438,462,486]
N = 16
ROUNDS = 6
def setup_inputs(rng):
    return {"x": rng.standard_normal((N, ROUNDS, 128, 16), dtype=np.float32)}
def reference(x):
    g = np.concatenate(list(x), axis=2)
    return {"y": np.broadcast_to(g, (N,) + g.shape)}

@@ -1,0 +1,90 @@
+import concourse.bass as bass
+
+SCRATCH = {
+    "d": ("dram", [18, 128, 32], "float32"),
+}
+SEMAPHORES = ["loc", "snd", "oa", "ob", "pq", "dd"]
+
+GENS = 3
+OWN, A, B, C, D, E, PEER = 0, 1, 2, 3, 4, 5, 6
+P_SLOT = (A, B, E)
+Q_SLOT = (C, D, C)
+D_SLOT = (E, A, D)
+LOW, HIGH = 0x0F, 0xF0
+
+
+def rank_program(g, core, T, topo):
+    rank = T.rank_of(core)
+    if rank is None:
+        return
+    h, ci = rank // 4, rank % 4
+    hosts = (h, h ^ 1, 3 - h, (3 - h) ^ 1)
+    cp, cq = T.cores[4 * hosts[1] + ci], T.cores[4 * hosts[2] + ci]
+    others = [c for c in range(4) if c != ci]
+    S, d = T.sem, T.d
+    n = {"loc": 0, "snd": 0}
+
+    def peer_slot(at, col, row):
+        return PEER + 4 * (col - (col > at)) + row
+
+    def dst(c):
+        rid, pid = topo.addr(c, core)
+        return bass.DstId(rid=rid, pnc=pid)
+
+    def local(out, in_):
+        g.dma_start(out=out, in_=in_).then_inc(S.loc, 16)
+        n["loc"] += 16
+
+    def store(t, slot, col, row):
+        j = 4 * hosts[row] + col
+        local(T.y[2 * t:2 * t + 2, :, 16 * j:16 * j + 16], d[slot])
+
+    def to_peers(row):
+        return [(T.cores[4 * h + c], peer_slot(c, ci, row)) for c in others]
+
+    def wave(moves):
+        g.wait_ge(S.snd, n["snd"])
+        g.wait_ge(S.loc, n["loc"])
+        g.remote_dma_fused([bass.RemoteDMATransfer(dst_ids=[dst(c) for c, s in to], dma_engine_mask=m, remote_sem=sem,
+                                                   srcs=[d[src]], dsts=[d[s] for c, s in to])
+                            for m, sem, src, to in moves], local_sem=S.snd)
+        n["snd"] += 4 * len(moves)
+
+    def take_pq(t):
+        g.wait_ge(S.pq, 28 * (t + 1))
+        store(t, D_SLOT[t], ci, 3)
+        for c in others:
+            store(t, peer_slot(ci, c, 1), c, 1)
+            store(t, peer_slot(ci, c, 2), c, 2)
+
+    def take_d(t):
+        g.wait_ge(S.dd, 12 * (t + 1))
+        for c in others:
+            store(t, peer_slot(ci, c, 3), c, 3)
+
+    def send_d(t):
+        return (LOW, S.dd, D_SLOT[t], to_peers(3))
+
+    local(T.y[:, :, 16 * rank:16 * rank + 16], T.x[:])
+    for t in range(GENS):
+        o_sem = S.ob if t % 2 else S.oa
+        if t:
+            take_pq(t - 1)
+            g.wait_ge(S.snd, n["snd"])
+        local(d[OWN], T.x[2 * t:2 * t + 2])
+        wave(([send_d(t - 1)] if t else []) +
+             [(HIGH, o_sem, OWN, [(cp, P_SLOT[t]), (cq, Q_SLOT[t])] + to_peers(0))])
+        if t:
+            take_d(t - 1)
+        g.wait_ge(o_sem, 20 * (t // 2 + 1))
+        store(t, P_SLOT[t], ci, 1)
+        store(t, Q_SLOT[t], ci, 2)
+        for c in others:
+            store(t, peer_slot(ci, c, 0), c, 0)
+        wave([(LOW, S.pq, Q_SLOT[t], [(cp, D_SLOT[t])] + to_peers(2)),
+              (HIGH, S.pq, P_SLOT[t], to_peers(1))])
+    take_pq(GENS - 1)
+    wave([send_d(GENS - 1)])
+    take_d(GENS - 1)
+    g.wait_ge(S.snd, n["snd"])
+    g.wait_ge(S.loc, n["loc"])

@@ -3,88 +3,121 @@ import concourse.bass as bass
 SCRATCH = {
     "d": ("dram", [18, 128, 32], "float32"),
 }
-SEMAPHORES = ["loc", "snd", "oa", "ob", "pq", "dd"]
+SEMAPHORES = ["loc", "snd", "w1", "w2", "w3", "w4", "w5", "w6", "w7"]
 
-GENS = 3
-OWN, A, B, C, D, E, PEER = 0, 1, 2, 3, 4, 5, 6
-P_SLOT = (A, B, E)
-Q_SLOT = (C, D, C)
-D_SLOT = (E, A, D)
-LOW, HIGH = 0x0F, 0xF0
+FLIP = {"P": 4, "Q": 12, "s": 2, "x": 1, "o": 3}
+ROW = {"O": 0, "P": 4, "Q": 12, "D": 8}
+
+WAVES = (
+    ((0, "O", "PQsx"), (1, "O", "Psx")),
+    ((0, "Q", "Psx"), (0, "P", "sx"), (0, "xO", "s"), (1, "xO", "s")),
+    ((0, "D", "xo"), (0, "xQ", "s"), (1, "O", "Q")),
+    ((1, "Q", "Psx"), (1, "P", "sx"), (0, "D", "s"), (0, "xP", "s")),
+    ((1, "D", "sx"), (1, "xP", "s"), (1, "xQ", "s"), (2, "O", "PQx")),
+    ((2, "Q", "Psx"), (2, "P", "sx"), (2, "xO", "s")),
+    ((2, "D", "sxo"), (2, "O", "s"), (2, "xP", "s"), (2, "xQ", "s"), (1, "xD", "s")),
+)
+SLOT = {
+    "O": (0, 1, 3), "P": (2, 3, 5), "Q": (4, 16, 12), "D": (9, 0, 14),
+    "sO": (5, 6, 4), "sP": (12, 2, 2), "sQ": (13, 7, 8), "sD": (8, 15, 13),
+    "xO": (7, 8, 1), "xP": (14, 4, 10), "xQ": (15, 13, 16), "xD": (5, 11, 0),
+    "oO": (10, 11, 7), "oP": (10, 6, 17), "oQ": (6, 17, 6), "oD": (17, 15, 9),
+}
+
+
+def name_at(piece, to):
+    if to == "Q":
+        return {"O": "Q"}[piece]
+    if to == "P":
+        return {"O": "P", "Q": "D"}[piece]
+    if len(piece) == 1:
+        return to + piece
+    return {"xs": "o"}[piece[0] + to] + piece[1]
+
+
+def origin(piece):
+    return ROW[piece[-1]] ^ (FLIP[piece[0]] if len(piece) == 2 else 0)
+
+
+def verify():
+    land, last, writer = {}, {}, {}
+    for w, calls in enumerate(WAVES, 1):
+        for t, piece, tos in calls:
+            if piece == "O":
+                land.setdefault((piece, t), w)
+            assert land[(piece, t)] < w or piece == "O"
+            last[(piece, t)] = w
+            for to in tos:
+                key = (name_at(piece, to), t)
+                assert key not in land
+                land[key], writer[key] = w, FLIP[to]
+    assert sorted(land) == sorted((p, t) for p in SLOT for t in range(3))
+
+    def heard(v, w):
+        known = set()
+        for u in range(v, w + 1):
+            known |= {a ^ FLIP[to] for a in known | {0} for t, piece, tos in WAVES[u - 1] for to in tos}
+        return known
+
+    for slot in range(18):
+        users = sorted((land[(p, t)], p, t) for p in SLOT for t in range(3) if SLOT[p][t] == slot)
+        for (wa, pa, ta), (wb, pb, tb) in zip(users, users[1:]):
+            free = last.get((pa, ta), wa) + 1
+            if pb == "O":
+                assert free <= wb - (0 if (pa, ta) in last else 1)
+            else:
+                assert writer[(pb, tb)] in heard(free, wb - 1)
+    return True
+
+
+VERIFIED = verify()
 
 
 def rank_program(g, core, T, topo):
     rank = T.rank_of(core)
     if rank is None:
         return
-    h, ci = rank // 4, rank % 4
-    hosts = (h, h ^ 1, 3 - h, (3 - h) ^ 1)
-    cp, cq = T.cores[4 * hosts[1] + ci], T.cores[4 * hosts[2] + ci]
-    others = [c for c in range(4) if c != ci]
     S, d = T.sem, T.d
+    arrived = (S.w1, S.w2, S.w3, S.w4, S.w5, S.w6, S.w7)
     n = {"loc": 0, "snd": 0}
 
-    def peer_slot(at, col, row):
-        return PEER + 4 * (col - (col > at)) + row
-
-    def dst(c):
-        rid, pid = topo.addr(c, core)
+    def dst(to):
+        rid, pid = topo.addr(T.cores[rank ^ FLIP[to]], core)
         return bass.DstId(rid=rid, pnc=pid)
 
     def local(out, in_):
         g.dma_start(out=out, in_=in_).then_inc(S.loc, 16)
         n["loc"] += 16
 
-    def store(t, slot, col, row):
-        j = 4 * hosts[row] + col
-        local(T.y[2 * t:2 * t + 2, :, 16 * j:16 * j + 16], d[slot])
+    def take(w):
+        calls = WAVES[w - 1]
+        g.wait_ge(arrived[w - 1], (8 // len(calls)) * sum(len(tos) for t, piece, tos in calls))
+        for t, piece, tos in calls:
+            for to in tos:
+                got = name_at(piece, to)
+                j = rank ^ origin(got)
+                local(T.y[2 * t:2 * t + 2, :, 16 * j:16 * j + 16], d[SLOT[got][t]])
 
-    def to_peers(row):
-        return [(T.cores[4 * h + c], peer_slot(c, ci, row)) for c in others]
-
-    def wave(moves):
+    loaded = set()
+    for w, calls in enumerate(WAVES, 1):
+        if w > 1:
+            take(w - 1)
         g.wait_ge(S.snd, n["snd"])
+        for t, piece, tos in calls:
+            if piece == "O" and t not in loaded:
+                loaded.add(t)
+                local(d[SLOT["O"][t]], T.x[2 * t:2 * t + 2])
         g.wait_ge(S.loc, n["loc"])
-        g.remote_dma_fused([bass.RemoteDMATransfer(dst_ids=[dst(c) for c, s in to], dma_engine_mask=m, remote_sem=sem,
-                                                   srcs=[d[src]], dsts=[d[s] for c, s in to])
-                            for m, sem, src, to in moves], local_sem=S.snd)
-        n["snd"] += 4 * len(moves)
-
-    def take_pq(t):
-        g.wait_ge(S.pq, 28 * (t + 1))
-        store(t, D_SLOT[t], ci, 3)
-        for c in others:
-            store(t, peer_slot(ci, c, 1), c, 1)
-            store(t, peer_slot(ci, c, 2), c, 2)
-
-    def take_d(t):
-        g.wait_ge(S.dd, 12 * (t + 1))
-        for c in others:
-            store(t, peer_slot(ci, c, 3), c, 3)
-
-    def send_d(t):
-        return (LOW, S.dd, D_SLOT[t], to_peers(3))
-
-    local(T.y[:, :, 16 * rank:16 * rank + 16], T.x[:])
-    for t in range(GENS):
-        o_sem = S.ob if t % 2 else S.oa
-        if t:
-            take_pq(t - 1)
-            g.wait_ge(S.snd, n["snd"])
-        local(d[OWN], T.x[2 * t:2 * t + 2])
-        wave(([send_d(t - 1)] if t else []) +
-             [(HIGH, o_sem, OWN, [(cp, P_SLOT[t]), (cq, Q_SLOT[t])] + to_peers(0))])
-        if t:
-            take_d(t - 1)
-        g.wait_ge(o_sem, 20 * (t // 2 + 1))
-        store(t, P_SLOT[t], ci, 1)
-        store(t, Q_SLOT[t], ci, 2)
-        for c in others:
-            store(t, peer_slot(ci, c, 0), c, 0)
-        wave([(LOW, S.pq, Q_SLOT[t], [(cp, D_SLOT[t])] + to_peers(2)),
-              (HIGH, S.pq, P_SLOT[t], to_peers(1))])
-    take_pq(GENS - 1)
-    wave([send_d(GENS - 1)])
-    take_d(GENS - 1)
+        k = 8 // len(calls)
+        g.remote_dma_fused([bass.RemoteDMATransfer(dst_ids=[dst(to) for to in tos],
+                                                   dma_engine_mask=((1 << k) - 1) << (k * i),
+                                                   remote_sem=arrived[w - 1],
+                                                   srcs=[d[SLOT[piece][t]]],
+                                                   dsts=[d[SLOT[name_at(piece, to)][t]] for to in tos])
+                            for i, (t, piece, tos) in enumerate(calls)], local_sem=S.snd)
+        n["snd"] += k * len(calls)
+        if w == 1:
+            local(T.y[:, :, 16 * rank:16 * rank + 16], T.x[:])
+    take(len(WAVES))
     g.wait_ge(S.snd, n["snd"])
     g.wait_ge(S.loc, n["loc"])

import concourse.bass as bass

SCRATCH = {
    "d": ("dram", [18, 128, 32], "float32"),
}
SEMAPHORES = ["loc", "snd", "w1", "w2", "w3", "w4", "w5", "w6", "w7"]

FLIP = {"P": 4, "Q": 12, "s": 2, "x": 1, "o": 3}
ROW = {"O": 0, "P": 4, "Q": 12, "D": 8}

WAVES = (
    ((0, "O", "PQsx"), (1, "O", "Psx")),
    ((0, "Q", "Psx"), (0, "P", "sx"), (0, "xO", "s"), (1, "xO", "s")),
    ((0, "D", "xo"), (0, "xQ", "s"), (1, "O", "Q")),
    ((1, "Q", "Psx"), (1, "P", "sx"), (0, "D", "s"), (0, "xP", "s")),
    ((1, "D", "sx"), (1, "xP", "s"), (1, "xQ", "s"), (2, "O", "PQx")),
    ((2, "Q", "Psx"), (2, "P", "sx"), (2, "xO", "s")),
    ((2, "D", "sxo"), (2, "O", "s"), (2, "xP", "s"), (2, "xQ", "s"), (1, "xD", "s")),
)
SLOT = {
    "O": (0, 1, 3), "P": (2, 3, 5), "Q": (4, 16, 12), "D": (9, 0, 14),
    "sO": (5, 6, 4), "sP": (12, 2, 2), "sQ": (13, 7, 8), "sD": (8, 15, 13),
    "xO": (7, 8, 1), "xP": (14, 4, 10), "xQ": (15, 13, 16), "xD": (5, 11, 0),
    "oO": (10, 11, 7), "oP": (10, 6, 17), "oQ": (6, 17, 6), "oD": (17, 15, 9),
}


def name_at(piece, to):
    if to == "Q":
        return {"O": "Q"}[piece]
    if to == "P":
        return {"O": "P", "Q": "D"}[piece]
    if len(piece) == 1:
        return to + piece
    return {"xs": "o"}[piece[0] + to] + piece[1]


def origin(piece):
    return ROW[piece[-1]] ^ (FLIP[piece[0]] if len(piece) == 2 else 0)


def verify():
    land, last, writer = {}, {}, {}
    for w, calls in enumerate(WAVES, 1):
        for t, piece, tos in calls:
            if piece == "O":
                land.setdefault((piece, t), w)
            assert land[(piece, t)] < w or piece == "O"
            last[(piece, t)] = w
            for to in tos:
                key = (name_at(piece, to), t)
                assert key not in land
                land[key], writer[key] = w, FLIP[to]
    assert sorted(land) == sorted((p, t) for p in SLOT for t in range(3))

    def heard(v, w):
        known = set()
        for u in range(v, w + 1):
            known |= {a ^ FLIP[to] for a in known | {0} for t, piece, tos in WAVES[u - 1] for to in tos}
        return known

    for slot in range(18):
        users = sorted((land[(p, t)], p, t) for p in SLOT for t in range(3) if SLOT[p][t] == slot)
        for (wa, pa, ta), (wb, pb, tb) in zip(users, users[1:]):
            free = last.get((pa, ta), wa) + 1
            if pb == "O":
                assert free <= wb - (0 if (pa, ta) in last else 1)
            else:
                assert writer[(pb, tb)] in heard(free, wb - 1)
    return True


VERIFIED = verify()


def rank_program(g, core, T, topo):
    rank = T.rank_of(core)
    if rank is None:
        return
    S, d = T.sem, T.d
    arrived = (S.w1, S.w2, S.w3, S.w4, S.w5, S.w6, S.w7)
    n = {"loc": 0, "snd": 0}

    def dst(to):
        rid, pid = topo.addr(T.cores[rank ^ FLIP[to]], core)
        return bass.DstId(rid=rid, pnc=pid)

    def local(out, in_):
        g.dma_start(out=out, in_=in_).then_inc(S.loc, 16)
        n["loc"] += 16

    def take(w):
        calls = WAVES[w - 1]
        g.wait_ge(arrived[w - 1], (8 // len(calls)) * sum(len(tos) for t, piece, tos in calls))
        for t, piece, tos in calls:
            for to in tos:
                got = name_at(piece, to)
                j = rank ^ origin(got)
                local(T.y[2 * t:2 * t + 2, :, 16 * j:16 * j + 16], d[SLOT[got][t]])

    loaded = set()
    for w, calls in enumerate(WAVES, 1):
        if w > 1:
            take(w - 1)
        g.wait_ge(S.snd, n["snd"])
        for t, piece, tos in calls:
            if piece == "O" and t not in loaded:
                loaded.add(t)
                local(d[SLOT["O"][t]], T.x[2 * t:2 * t + 2])
        g.wait_ge(S.loc, n["loc"])
        k = 8 // len(calls)
        g.remote_dma_fused([bass.RemoteDMATransfer(dst_ids=[dst(to) for to in tos],
                                                   dma_engine_mask=((1 << k) - 1) << (k * i),
                                                   remote_sem=arrived[w - 1],
                                                   srcs=[d[SLOT[piece][t]]],
                                                   dsts=[d[SLOT[name_at(piece, to)][t]] for to in tos])
                            for i, (t, piece, tos) in enumerate(calls)], local_sem=S.snd)
        n["snd"] += k * len(calls)
        if w == 1:
            local(T.y[:, :, 16 * rank:16 * rank + 16], T.x[:])
    take(len(WAVES))
    g.wait_ge(S.snd, n["snd"])
    g.wait_ge(S.loc, n["loc"])
